import numpy as np
import ml_dtypes


def mxq(x, axis, fmt="e4m3"):
    dtype, down = {"e4m3": (ml_dtypes.float8_e4m3fn, 7), "e5m2": (ml_dtypes.float8_e5m2, 14)}[fmt]
    v = np.moveaxis(np.asarray(x, np.float32).astype(ml_dtypes.bfloat16).astype(np.float64), axis, -1)
    blocks = v.reshape(v.shape[:-1] + (-1, 32))
    amax = np.abs(blocks).max(-1, keepdims=True)
    byte = np.maximum(np.where(amax > 0, np.frexp(amax)[1] - 1 + 127, 0) - down, 1)
    scale = np.exp2(byte - 127.0)
    codes = (blocks / scale).astype(np.float32).astype(dtype).astype(np.float64)
    return np.moveaxis((codes * scale).reshape(v.shape), -1, axis)


WIDE = False


def mx_kscale(k):
    if not WIDE:
        return np.ones(k)
    levels = np.array([10, -10, 5, -5, 0])
    if k % 512:
        return np.exp2(np.random.permutation(np.resize(levels, k // 32))).repeat(32)
    a = np.empty((k // 512, 16))
    for p in range(k // 512):
        a[p, :8] = np.random.permutation(np.resize(levels, 8))
        for g in range(8):
            far = levels[np.abs(levels - a[p, g]) >= 10]
            a[p, g + 8] = far[np.random.randint(len(far))]
    return np.exp2(a.ravel()).repeat(32)


BF16 = ml_dtypes.bfloat16


def bf(x):
    return np.asarray(x, np.float32).astype(BF16)


def f64(x):
    return np.asarray(x).astype(np.float64)


E2M1 = np.array([0.0, 0.5, 1.0, 1.5, 2.0, 3.0, 4.0, 6.0, -0.0, -0.5, -1.0, -1.5, -2.0, -3.0, -4.0, -6.0])


def pack_weight(w, fmt):
    k, n = w.shape
    w = f64(bf(w)).reshape(k // 32, 32, n)
    amax = np.abs(w).max(1)
    if fmt == "e4m3":
        byte = np.frexp(amax)[1] - 1 + 127 - 7
    else:
        mant, ex = np.frexp(amax / 6.0)
        byte = np.where(mant > 0.5, ex, ex - 1) + 127
    byte = np.clip(np.where(amax > 0, byte, 1), 1, 254)
    scaled = (w * np.exp2(127.0 - byte)[:, None, :]).reshape(k, n).astype(np.float32)
    by_word = np.ascontiguousarray(scaled.reshape(k // 512, 128, 4, n).transpose(0, 1, 3, 2))
    if fmt == "e4m3":
        words = by_word.astype(ml_dtypes.float8_e4m3fn).view(np.uint8)
    else:
        c = by_word.astype(ml_dtypes.float4_e2m1fn).view(np.uint8) & 0xF
        words = c[..., 0::2] | (c[..., 1::2] << 4)
    return np.ascontiguousarray(words), np.ascontiguousarray(byte.astype(np.uint8).reshape(k // 512, 16, n))


def unpack_weight(words, scales, fmt):
    g, p, n, _ = words.shape
    if fmt == "e4m3":
        vals = np.ascontiguousarray(words).view(ml_dtypes.float8_e4m3fn).astype(np.float64)
    else:
        nib = np.empty((g, p, n, 4), np.uint8)
        nib[..., 0::2] = words & 0xF
        nib[..., 1::2] = words >> 4
        vals = E2M1[nib]
    vals = vals * np.repeat(np.exp2(scales.astype(np.float64) - 127.0), 8, axis=1)[..., None]
    return vals.transpose(0, 1, 3, 2).reshape(g * 512, n)

E4M3FN = np.array([(-1.0 if i & 128 else 1.0) * ((1.0 + (i & 7) / 8.0) * 2.0 ** (((i >> 3) & 15) - 7) if i & 120 else (i & 7) * 2.0 ** -9) for i in range(256)])


def e4m3fn_bytes(y):
    return np.clip(np.asarray(y, np.float64), -448.0, 448.0).astype(np.float32).astype(ml_dtypes.float8_e4m3fn).view(np.uint8)


def e4m3fn_values(b):
    return E4M3FN[b]


B, DI, D = 1024, 512, 512


def sigmoid(v):
    return 1.0 / (1.0 + np.exp(-v))


def draw0():
    p, q = mx_kscale(DI), mx_kscale(D)
    x = bf(np.random.standard_normal((B, DI)) * p)
    h = bf(np.random.standard_normal((B, D)) * 0.5)
    t = bf(np.random.standard_normal((B, D)))
    wx_words, wx_scales = pack_weight(np.random.standard_normal((DI, 4 * D)) / np.sqrt(DI) / p[:, None], "e4m3")
    uh = bf(np.random.standard_normal((D, 2 * D)) * 2.0 / np.sqrt(D))
    g = bf((1.0 + 0.1 * np.random.standard_normal(D)) * q)
    un_words, un_scales = pack_weight(np.random.standard_normal((D, D)) * 3.0 / np.sqrt(D) / q[:, None], "e4m3")
    return {
        "x": x,
        "h": h,
        "t": t,
        "wx_words": wx_words,
        "wx_scales": wx_scales,
        "uh": uh,
        "g": g,
        "un_words": un_words,
        "un_scales": un_scales,
    }


def core(x, h, t, wx_words, wx_scales, uh, g, un_words, un_scales):
    d = h.shape[-1]
    hf = f64(h)

    gx = mxq(f64(x), 1, "e4m3") @ unpack_weight(wx_words, wx_scales, "e4m3")
    xa = gx[:, :d]
    xu = gx[:, d:2 * d]
    xr = gx[:, 2 * d:3 * d]
    xn = gx[:, 3 * d:]

    gh = f64(h) @ f64(uh)
    hu = gh[:, :d]
    hr = gh[:, d:]

    a = sigmoid(np.sum(xa * f64(t), axis=-1) / np.sqrt(d))

    u = sigmoid(xu + hu)
    r = sigmoid(xr + hr)

    s = r * hf * f64(g)[None, :]

    n = np.tanh(xn + (mxq(s, 1, "e4m3") @ unpack_weight(un_words, un_scales, "e4m3")))

    ua = a[:, None] * u

    return (1.0 - ua) * hf + ua * n


def setup_inputs():
    drawn = draw0()
    full = np.asarray(drawn['x']).astype(np.float64)
    scale = (np.abs(full).reshape(1024, 4, 128).max(axis=(2,)) / 448.0).astype(np.float32)
    given = {}
    for key, value in drawn.items():
        if key == 'x':
            given['x_bytes'] = e4m3fn_bytes(full / np.repeat(scale.astype(np.float64), 128, axis=1))
            given['x_scale'] = scale
        else:
            given[key] = value
    return given


def reference(x_bytes, x_scale, h, t, wx_words, wx_scales, uh, g, un_words, un_scales):
    return core(e4m3fn_values(x_bytes) * np.repeat(x_scale.astype(np.float64), 128, axis=1), h, t, wx_words, wx_scales, uh, g, un_words, un_scales)

@@ -1,0 +1,276 @@
+from contextlib import ExitStack
+
+import concourse.mybir as mybir
+from concourse.masks import make_identity
+
+B, DI, D = 1024, 512, 512
+FLOPS = 2 * B * DI * 4 * D + 2 * B * D * 2 * D + 2 * B * D * D
+
+F32 = mybir.dt.float32
+BF16 = mybir.dt.bfloat16
+I32 = mybir.dt.int32
+U32 = mybir.dt.uint32
+U8 = mybir.dt.uint8
+FP8 = mybir.dt.float8_e4m3fn
+X4 = mybir.dt.float8_e4m3fn_x4
+ALU = mybir.AluOpType
+ACT = mybir.ActivationFunctionType
+
+P = 128
+NT = 8
+NQ = 4
+MANUAL = True
+W_ACT = ["W00","W21","W31"]
+IS_ACT = ["IS0","IS3"]
+D3_GP = ["DC00","DC01","DC10","DC11","DC20","DC21","DC30"]
+LOADS = ["h0","x01","uhu","h1","uhr","h3","un","x23","wx2","wx1","wx3","t23","h2","wx0","t01"]
+SEQ = (
+    "W00 W01 Th0 CH0 PERMa Tx0 CX0 QX0 PERMb PERM W10 W20 W30 HU01 CU01 HU00 "
+    "CU00 Th1 W11 W21 CH1 HR00 CR00 HR01 CR01 PERMW XR00 AR00 SR00 XR01 AR01 SR01 "
+    "Tx1 CX1 XU00 AU00 SU00 HR10 CR10 S00 S01 IS0 XA00 AA00 HR11 CR11 QX1 XU01 "
+    "AU01 XA01 AA01 SA0 Th2 CH2 XR10 AR10 SR10 QS0 XR11 AR11 SR11 XA10 AA10 HU11 "
+    "CU11 SU01 S10 XU10 HR20 CR20 S11 IS1 QS1 N00 TN00 DA00 N01 TN01 DA01 Tx2 "
+    "CX2 QX2 DB01 DC01 HU10 CU10 AU10 XA11 AA11 SA1 HR21 CR21 XR20 AR20 SR20 HU20 "
+    "DB00 DC00 W31 XR21 AR21 SR21 XA21 XA20 AA20 AA21 XU21 S21 S20 IS2 QS2 CU20 "
+    "Th3 CH3 N10 TN10 DA10 Tx3 CX3 QX3 N11 TN11 HU21 CU21 AU21 XU11 AU11 SU10 "
+    "DB10 DC10 HR31 CR31 HR30 CR30 XU20 AU20 SU20 XR30 AR30 SR30 XR31 AR31 SR31 XA30 "
+    "AA30 DA11 S30 SA2 S31 SU11 DB11 HU30 CU30 HU31 CU31 XU30 AU30 DC11 XA31 AA31 "
+    "XU31 AU31 IS3 QS3 N20 TN20 DA20 N21 TN21 DA21 N30 DB20 SU30 SU21 DB21 DC21 "
+    "TN30 DA30 DC20 N31 TN31 DA31 SA3 DB30 DC30 SU31 DB31 DC31 "
+)
+
+
+def tile_dienaugrustep_d1p_kernel(tc, x_bytes, x_scale, h, t, wx_words, wx_scales, uh, g, un_words, un_scales, out):
+    nc = tc.nc
+    with ExitStack() as ctx:
+        keep = ctx.enter_context(tc.tile_pool(name="keep", bufs=1))
+        work = ctx.enter_context(tc.tile_pool(name="work", bufs=4))
+        psum_t = ctx.enter_context(tc.psum_pool(name="psum_t", bufs=2))
+        psum_h = ctx.enter_context(tc.psum_pool(name="psum_h", bufs=2))
+        psum_m = ctx.enter_context(tc.psum_pool(name="psum_m", bufs=4))
+        if MANUAL:
+            ctx.enter_context(tc.manual_schedule())
+
+        ident = keep.tile([P, P], F32, name="ident")
+        warm = keep.tile([P, 1], F32, name="warm")
+        warm_out = keep.tile([P, 1], F32, name="warm_out")
+        xs = keep.tile([P, NT * 4], F32, name="xs")
+        x_u8 = keep.tile([P, NT, DI], U8, name="x_u8")
+        xb = keep.tile([P, NT, DI], BF16, name="xb", align_bytes=64)
+        xc = keep.tile([P, B], U32, name="xc", align_bytes=64)
+        xsc = keep.tile([P, B], U8, name="xsc", align_bytes=64)
+        h_sb = keep.tile([P, NT, D], BF16, name="h_sb")
+        t_sb = keep.tile([P, NT, D], BF16, name="t_sb")
+        hT = keep.tile([P, 4, B], BF16, name="hT")
+        uhu = keep.tile([P, 4, D], BF16, name="uhu")
+        uhr_raw = keep.tile([P, 4, D], BF16, name="uhr_raw")
+        uhr = keep.tile([P, 4, 4, P], BF16, name="uhr")
+        wx = [keep.tile([P, 512], U32, name="wx%d" % b, align_bytes=64) for b in range(4)]
+        wxs = keep.tile([P, 2048], U8, name="wxs", align_bytes=64)
+        wr = keep.tile([P, 512], U32, name="wr", align_bytes=64)
+        wrs = keep.tile([P, 512], U8, name="wrs", align_bytes=64)
+        un = keep.tile([P, 512], U32, name="un", align_bytes=64)
+        uns = keep.tile([P, 512], U8, name="uns", align_bytes=64)
+        g_bf = keep.tile([P, 4], BF16, name="g_bf")
+        g32 = keep.tile([P, 4], F32, name="g32")
+        dot = keep.tile([P, NT], F32, name="dot")
+        att = keep.tile([P, NT], F32, name="att")
+
+        nc.vector.memset(warm[:], 0.0)
+        nc.scalar.activation(warm_out[:], warm[:], ACT.Sigmoid)
+        nc.vector.memset(wxs[:].bitcast(I32), 0)
+        nc.vector.memset(uns[:].bitcast(I32), 0)
+        make_identity(nc, ident[:])
+
+        x_v = x_bytes.rearrange("(p j) k -> p j k", j=NT)
+        h_v = h.rearrange("(p j) c -> p j c", j=NT)
+        t_v = t.rearrange("(p j) c -> p j c", j=NT)
+        o_v = out.rearrange("(p j) c -> p j c", j=NT)
+        uh_v = uh.rearrange("(p s) n -> p s n", s=4)
+        wx_v = wx_words[0].rearrange("p n t -> p (n t)")
+        un_v = un_words[0].rearrange("p n t -> p (n t)")
+
+        nc.scalar.dma_start(out=xs[:], in_=x_scale.rearrange("(p j) b -> p (j b)", j=NT))
+        for q in range(4):
+            nc.scalar.dma_start(out=wxs[32 * q : 32 * q + 4, :].bitcast(I32), in_=wx_scales[0][4 * q : 4 * q + 4, :].bitcast(I32))
+        nc.scalar.dma_start(out=g_bf[:], in_=g.rearrange("(p s) -> p s", s=4))
+        for q in range(4):
+            nc.scalar.dma_start(out=uns[32 * q : 32 * q + 4, :].bitcast(I32), in_=un_scales[0][4 * q : 4 * q + 4, :].bitcast(I32))
+
+        def load_h(q):
+            nc.sync.dma_start(out=h_sb[:, 2 * q : 2 * q + 2, :], in_=h_v[:, 2 * q : 2 * q + 2, :])
+
+        def load_t(k):
+            nc.sync.dma_start(out=t_sb[:, 4 * k : 4 * k + 4, :], in_=t_v[:, 4 * k : 4 * k + 4, :])
+
+        def load_x(k):
+            nc.sync.dma_start(out=x_u8[:, 4 * k : 4 * k + 4, :], in_=x_v[:, 4 * k : 4 * k + 4, :])
+
+        def load_w(b):
+            nc.sync.dma_start(out=wx[b][:].bitcast(I32), in_=wx_v[:, 2048 * b : 2048 * b + 2048].bitcast(I32))
+
+
+        def load(name):
+            if name[0] == "x":
+                load_x(0 if name == "x01" else 1)
+            elif name[0] == "h":
+                load_h(int(name[1]))
+            elif name[0] == "t":
+                load_t(0 if name == "t01" else 1)
+            elif name == "uhu":
+                nc.sync.dma_start(out=uhu[:], in_=uh_v[:, :, 0:512])
+            elif name == "uhr":
+                nc.sync.dma_start(out=uhr_raw[:], in_=uh_v[:, :, 512:1024])
+            elif name == "un":
+                nc.sync.dma_start(out=un[:].bitcast(I32), in_=un_v.bitcast(I32))
+            else:
+                load_w(int(name[2]))
+
+        for name in LOADS:
+            load(name)
+
+        hu_sb = [keep.tile([P, 2, D], F32, name="hu_sb%d" % q) for q in range(NQ)]
+        hr_sb = [keep.tile([P, 2, D], F32, name="hr_sb%d" % q) for q in range(NQ)]
+        u_sb = [keep.tile([P, 2, D], F32, name="u_sb%d" % q) for q in range(NQ)]
+        r_sb = [keep.tile([P, 2, D], F32, name="r_sb%d" % q) for q in range(NQ)]
+        su = [keep.tile([P, 4, 256], BF16, name="su%d" % q) for q in range(NQ)]
+        sg = [keep.tile([P, 1024], BF16, name="sg%d" % q, align_bytes=64) for q in range(NQ)]
+        xg = [keep.tile([P, 1024], BF16, name="xg%d" % q, align_bytes=64) for q in range(NQ)]
+        sc = [keep.tile([P, 256], U32, name="sc%d" % q, align_bytes=64) for q in range(NQ)]
+        ss = [keep.tile([P, 256], U8, name="ss%d" % q, align_bytes=64) for q in range(NQ)]
+        bank, part = {}, {}
+
+        def transposes(src, q):
+            pt = psum_t.tile([P, 2, 2, P], F32, name="tp", tag="tp")
+            for i in range(2):
+                words = src[:, 2 * q + i, :].bitcast(F32)
+                for u in range(2):
+                    nc.tensor.transpose(pt[:, i, u, :], words[:, u:256:2], ident[:])
+            return pt
+
+        def x_block(ps, j, b, start, stop):
+            tok = slice(128 * j, 128 * j + 128)
+            nc.tensor.matmul_mx(ps[:], lhsT=xc[:, tok].bitcast(X4), lhsT_scale=xsc[:, tok], rhs=wx[b][:].bitcast(X4), rhs_scale=wxs[:, 512 * b : 512 * b + 512], start=start, stop=stop)
+
+        def mxbank():
+            return psum_m.tile([P, D], F32, name="mx", tag="mx")
+
+        def emit(name):
+            op = "".join([c for c in name if c not in "0123456789"])
+            dig = name[len(op):]
+            q = int(dig[0]) if dig else 0
+            i = int(dig[1]) if len(dig) > 1 else 0
+            j = 2 * q + i
+            cols = slice(256 * q, 256 * q + 256)
+            key = (q, i)
+            if op == "Th":
+                bank["h", q] = transposes(h_sb, q)
+            elif op == "CH":
+                pt = bank["h", q]
+                pv = pt[:].rearrange("p i u r -> p (i u r)").bitcast(BF16).rearrange("p (i u r e) -> p u e i r", i=2, u=2, e=2)
+                for u in range(2):
+                    o = hT[:, 2 * u : 2 * u + 2, cols].rearrange("p e (i r) -> p e i r", i=2)
+                    nc.scalar.copy(o, pv[:, u])
+            elif op == "W":
+                for b in range(4):
+                    src = x_u8[:, j, 128 * b : 128 * b + 128].bitcast(FP8)
+                    dst = xb[:, j, 128 * b : 128 * b + 128]
+                    sca = xs[:, 4 * j + b : 4 * j + b + 1]
+                    if name in W_ACT:
+                        nc.scalar.activation(dst, src, ACT.Copy, scale=sca)
+                    else:
+                        nc.vector.tensor_scalar(out=dst, in0=src, scalar1=sca, scalar2=None, op0=ALU.mult)
+            elif op == "Tx":
+                bank["x", q] = transposes(xb, q)
+            elif op == "CX":
+                nc.scalar.copy(xg[q][:].bitcast(F32).rearrange("p (i r u) -> p i r u", i=2, u=2), bank["x", q][:].rearrange("p i u r -> p i r u"))
+            elif op == "QX":
+                nc.vector.quantize_mx(out=xc[:, cols].bitcast(X4), scales=xsc[:, cols], in_=xg[q][:])
+            elif op == "PERMa":
+                for s in range(3):
+                    nc.vector.tensor_copy(out=uhr[:, s], in_=uhr_raw[:, s, :].rearrange("p (m c) -> p c m", c=4))
+            elif op == "PERMb":
+                nc.scalar.copy(uhr[:, 3], uhr_raw[:, 3, :].rearrange("p (m c) -> p c m", c=4))
+            elif op == "PERM":
+                nc.vector.tensor_copy(out=g32[:], in_=g_bf[:])
+            elif op == "PERMW":
+                nc.vector.tensor_copy(out=wr[:].bitcast(I32).rearrange("p (c m) -> p c m", c=4), in_=wx[2][:].bitcast(I32).rearrange("p (m c) -> p c m", c=4))
+                nc.vector.tensor_copy(out=wrs[:].rearrange("p (c m) -> p m c", c=4), in_=wxs[:, 1024:1536].rearrange("p (m c) -> p m c", c=4))
+            elif op == "HU":
+                ps = psum_h.tile([P, D], F32, name="hp", tag="hp")
+                bank["hu", key] = ps
+                for s in range(4):
+                    nc.tensor.matmul(ps[:], lhsT=hT[:, s, 128 * j : 128 * j + 128], rhs=uhu[:, s, :], start=(s == 0), stop=(s == 3))
+            elif op == "CU":
+                nc.scalar.copy(hu_sb[q][:, i, :], bank["hu", key][:])
+            elif op == "HR":
+                ps = psum_h.tile([P, D], F32, name="hp", tag="hp")
+                bank["hr", key] = ps
+                for w in range(2):
+                    for s in range(4):
+                        nc.tensor.matmul(ps[:, 256 * w : 256 * w + 256], lhsT=uhr[:, s, 2 * i + w, :], rhs=hT[:, s, cols], start=(s == 0), stop=(s == 3))
+            elif op == "CR":
+                nc.scalar.copy(hr_sb[q][:, i, :], bank["hr", key][:])
+            elif op == "XR":
+                ps = mxbank()
+                bank["xr", key] = ps
+                for w in range(2):
+                    ch = slice(128 * (2 * i + w), 128 * (2 * i + w) + 128)
+                    nc.tensor.matmul_mx(ps[:, 256 * w : 256 * w + 256], lhsT=wr[:, ch].bitcast(X4), lhsT_scale=wrs[:, ch], rhs=xc[:, cols].bitcast(X4), rhs_scale=xsc[:, cols], start=True, stop=True)
+            elif op == "AR":
+                part["rp", key] = work.tile([P, D], F32, name="rp")
+                nc.vector.tensor_tensor(out=part["rp", key][:], in0=bank["xr", key][:], in1=hr_sb[q][:, i, :], op=ALU.add)
+            elif op == "SR":
+                nc.scalar.activation(r_sb[q][:, i, :], part["rp", key][:], ACT.Sigmoid)
+            elif op == "S":
+                for w in range(2):
+                    c = 2 * i + w
+                    nc.vector.scalar_tensor_tensor(out=su[q][:, c, :], in0=r_sb[q][:, i, 256 * w : 256 * w + 256], scalar=g32[:, c : c + 1], in1=hT[:, c, cols], op0=ALU.mult, op1=ALU.mult)
+            elif op == "IS":
+                o, s_ = sg[q][:].rearrange("p (c t) -> p c t", t=4), su[q][:].rearrange("p t c -> p c t")
+                if name in IS_ACT:
+                    nc.scalar.copy(o, s_)
+                else:
+                    nc.vector.tensor_copy(out=o, in_=s_)
+            elif op == "QS":
+                nc.vector.quantize_mx(out=sc[q][:].bitcast(X4), scales=ss[q][:], in_=sg[q][:])
+            elif op == "XU":
+                bank["xu", key] = mxbank()
+                x_block(bank["xu", key], j, 1, True, True)
+            elif op == "AU":
+                part["up", key] = work.tile([P, D], F32, name="up")
+                nc.vector.tensor_tensor(out=part["up", key][:], in0=bank["xu", key][:], in1=hu_sb[q][:, i, :], op=ALU.add)
+            elif op == "SU":
+                nc.scalar.activation(u_sb[q][:, i, :], part["up", key][:], ACT.Sigmoid)
+            elif op == "XA":
+                bank["xa", key] = mxbank()
+                x_block(bank["xa", key], j, 0, True, True)
+            elif op == "AA":
+                prod = work.tile([P, D], F32, name="prod")
+                nc.vector.scalar_tensor_tensor(out=prod[:], in0=bank["xa", key][:], scalar=1.0, in1=t_sb[:, j, :], op0=ALU.mult, op1=ALU.mult, accum_out=dot[:, j : j + 1])
+            elif op == "SA":
+                nc.scalar.activation(att[:, 2 * q : 2 * q + 2], dot[:, 2 * q : 2 * q + 2], ACT.Sigmoid, scale=1.0 / (512.0**0.5))
+            elif op == "N":
+                bank["n", key] = mxbank()
+                x_block(bank["n", key], j, 3, True, False)
+                tok = slice(128 * i, 128 * i + 128)
+                nc.tensor.matmul_mx(bank["n", key][:], lhsT=sc[q][:, tok].bitcast(X4), lhsT_scale=ss[q][:, tok], rhs=un[:].bitcast(X4), rhs_scale=uns[:], start=False, stop=True)
+            elif op == "TN":
+                part["n", key] = work.tile([P, D], F32, name="n")
+                nc.scalar.activation(part["n", key][:], bank["n", key][:], ACT.Tanh)
+            elif op == "DA":
+                part["d", key] = work.tile([P, D], F32, name="d")
+                nc.vector.tensor_tensor(out=part["d", key][:], in0=part["n", key][:], in1=h_sb[:, j, :], op=ALU.subtract)
+            elif op == "DB":
+                part["e", key] = work.tile([P, D], F32, name="e")
+                nc.vector.scalar_tensor_tensor(out=part["e", key][:], in0=part["d", key][:], scalar=att[:, j : j + 1], in1=u_sb[q][:, i, :], op0=ALU.mult, op1=ALU.mult)
+            elif op == "DC":
+                o = work.tile([P, D], F32, name="o")
+                if name in D3_GP:
+                    nc.gpsimd.tensor_tensor(out=o[:], in0=part["e", key][:], in1=h_sb[:, j, :], op=ALU.add)
+                else:
+                    nc.vector.tensor_tensor(out=o[:], in0=part["e", key][:], in1=h_sb[:, j, :], op=ALU.add)
+                nc.sync.dma_start(out=o_v[:, j, :], in_=o[:])
+
+        for name in SEQ.split():
+            emit(name)

@@ -20,23 +20,23 @@ P = 128
 NT = 8
 NQ = 4
 MANUAL = True
-W_ACT = ["W00","W21","W31"]
-IS_ACT = ["IS0","IS3"]
-D3_GP = ["DC00","DC01","DC10","DC11","DC20","DC21","DC30"]
-LOADS = ["h0","x01","uhu","h1","uhr","h3","un","x23","wx2","wx1","wx3","t23","h2","wx0","t01"]
+W_ACT = ["W00","W01","W11","W20","W21","W30","W31"]
+IS_ACT = ["IS1","IS2","IS3"]
+D3_GP = []
+LOADS = ["x01","h0","uha","uhb","x23","wx2","h3","h1","wx0","wx1","h2","un","t01","wx3","t23"]
 SEQ = (
-    "W00 W01 Th0 CH0 PERMa Tx0 CX0 QX0 PERMb PERM W10 W20 W30 HU01 CU01 HU00 "
-    "CU00 Th1 W11 W21 CH1 HR00 CR00 HR01 CR01 PERMW XR00 AR00 SR00 XR01 AR01 SR01 "
-    "Tx1 CX1 XU00 AU00 SU00 HR10 CR10 S00 S01 IS0 XA00 AA00 HR11 CR11 QX1 XU01 "
-    "AU01 XA01 AA01 SA0 Th2 CH2 XR10 AR10 SR10 QS0 XR11 AR11 SR11 XA10 AA10 HU11 "
-    "CU11 SU01 S10 XU10 HR20 CR20 S11 IS1 QS1 N00 TN00 DA00 N01 TN01 DA01 Tx2 "
-    "CX2 QX2 DB01 DC01 HU10 CU10 AU10 XA11 AA11 SA1 HR21 CR21 XR20 AR20 SR20 HU20 "
-    "DB00 DC00 W31 XR21 AR21 SR21 XA21 XA20 AA20 AA21 XU21 S21 S20 IS2 QS2 CU20 "
-    "Th3 CH3 N10 TN10 DA10 Tx3 CX3 QX3 N11 TN11 HU21 CU21 AU21 XU11 AU11 SU10 "
-    "DB10 DC10 HR31 CR31 HR30 CR30 XU20 AU20 SU20 XR30 AR30 SR30 XR31 AR31 SR31 XA30 "
-    "AA30 DA11 S30 SA2 S31 SU11 DB11 HU30 CU30 HU31 CU31 XU30 AU30 DC11 XA31 AA31 "
-    "XU31 AU31 IS3 QS3 N20 TN20 DA20 N21 TN21 DA21 N30 DB20 SU30 SU21 DB21 DC21 "
-    "TN30 DA30 DC20 N31 TN31 DA31 SA3 DB30 DC30 SU31 DB31 DC31 "
+    "PERMa PERMc W01 W00 W11 W10 Th0 CH0 PERMb PERM W21 W20 Tx0 CX0 PERMW HU01 "
+    "CU01 HR00 CR00 QX0 HR01 CR01 XR00 AR00 XR01 AR01 XU01 AU01 SR00 S00 SR01 S01 "
+    "Th1 CH1 HU00 CU00 W31 IS0 QS0 XU00 AU00 XA01 AA01 XA00 AA00 W30 Tx1 CX1 "
+    "HR10 CR10 QX1 N00 TN00 DA00 N01 TN01 DA01 SU00 HR11 CR11 XR10 AR10 XR11 AR11 "
+    "SA0 DB00 XU10 SU01 SR10 S10 SR11 S11 HU10 CU10 AU10 Th2 CH2 DB01 XA11 AA11 "
+    "IS1 QS1 XU11 DC00 XA10 AA10 HU11 CU11 AU11 Tx2 CX2 DC01 HR20 CR20 QX2 N10 "
+    "TN10 DA10 N11 TN11 DA11 SU10 HR21 CR21 XR20 AR20 XR21 AR21 SA1 DB10 XU20 SU11 "
+    "SR20 S20 SR21 S21 HU20 CU20 AU20 Th3 CH3 DB11 XA21 AA21 IS2 QS2 XU21 DC10 "
+    "XA20 AA20 HU21 CU21 AU21 Tx3 CX3 DC11 QX3 HR30 CR30 N20 TN20 DA20 N21 TN21 "
+    "DA21 SU20 HR31 CR31 XR30 AR30 XR31 AR31 SA2 DB20 SU21 SR30 S30 SR31 S31 DB21 "
+    "HU30 CU30 XA31 AA31 XU30 AU30 XU31 IS3 QS3 DC20 XA30 AA30 HU31 CU31 AU31 DC21 "
+    "N30 TN30 DA30 N31 TN31 DA31 SU30 SA3 DB30 SU31 DB31 DC30 DC31 "
 )
 
 
@@ -45,14 +45,13 @@ def tile_dienaugrustep_d1p_kernel(tc, x_bytes, x_scale, h, t, wx_words, wx_scale
     with ExitStack() as ctx:
         keep = ctx.enter_context(tc.tile_pool(name="keep", bufs=1))
         work = ctx.enter_context(tc.tile_pool(name="work", bufs=4))
-        psum_t = ctx.enter_context(tc.psum_pool(name="psum_t", bufs=2))
-        psum_h = ctx.enter_context(tc.psum_pool(name="psum_h", bufs=2))
+        psum_t = ctx.enter_context(tc.psum_pool(name="psum_t", bufs=1))
+        psum_h = ctx.enter_context(tc.psum_pool(name="psum_h", bufs=3))
         psum_m = ctx.enter_context(tc.psum_pool(name="psum_m", bufs=4))
         if MANUAL:
             ctx.enter_context(tc.manual_schedule())
 
         ident = keep.tile([P, P], F32, name="ident")
-        warm = keep.tile([P, 1], F32, name="warm")
         warm_out = keep.tile([P, 1], F32, name="warm_out")
         xs = keep.tile([P, NT * 4], F32, name="xs")
         x_u8 = keep.tile([P, NT, DI], U8, name="x_u8")
@@ -62,8 +61,7 @@ def tile_dienaugrustep_d1p_kernel(tc, x_bytes, x_scale, h, t, wx_words, wx_scale
         h_sb = keep.tile([P, NT, D], BF16, name="h_sb")
         t_sb = keep.tile([P, NT, D], BF16, name="t_sb")
         hT = keep.tile([P, 4, B], BF16, name="hT")
-        uhu = keep.tile([P, 4, D], BF16, name="uhu")
-        uhr_raw = keep.tile([P, 4, D], BF16, name="uhr_raw")
+        uh_sb = keep.tile([P, 4, 2 * D], BF16, name="uh_sb")
         uhr = keep.tile([P, 4, 4, P], BF16, name="uhr")
         wx = [keep.tile([P, 512], U32, name="wx%d" % b, align_bytes=64) for b in range(4)]
         wxs = keep.tile([P, 2048], U8, name="wxs", align_bytes=64)
@@ -76,11 +74,21 @@ def tile_dienaugrustep_d1p_kernel(tc, x_bytes, x_scale, h, t, wx_words, wx_scale
         dot = keep.tile([P, NT], F32, name="dot")
         att = keep.tile([P, NT], F32, name="att")
 
-        nc.vector.memset(warm[:], 0.0)
-        nc.scalar.activation(warm_out[:], warm[:], ACT.Sigmoid)
         nc.vector.memset(wxs[:].bitcast(I32), 0)
-        nc.vector.memset(uns[:].bitcast(I32), 0)
+        nc.scalar.dma_start(out=xs[:], in_=x_scale.rearrange("(p j) b -> p (j b)", j=NT))
+        for q in range(4):
+            nc.scalar.dma_start(out=wxs[32 * q : 32 * q + 4, :].bitcast(I32), in_=wx_scales[0][4 * q : 4 * q + 4, :].bitcast(I32))
+        ones = keep.tile([P, 256], BF16, name="ones")
+        nc.gpsimd.memset(ones[:], 1.0)
+        nc.scalar.activation(warm_out[:], ones[:, 0:1], ACT.Sigmoid)
         make_identity(nc, ident[:])
+        nc.gpsimd.memset(uns[:].bitcast(I32), 0)
+        nc.gpsimd.dma_start(out=g_bf[:], in_=g.rearrange("(p s) -> p s", s=4))
+        for q in range(4):
+            nc.gpsimd.dma_start(out=uns[32 * q : 32 * q + 4, :].bitcast(I32), in_=un_scales[0][4 * q : 4 * q + 4, :].bitcast(I32))
+        wps = psum_t.tile([P, 256], F32, name="tp", tag="tp")
+        for k in range(8):
+            nc.tensor.matmul(wps[:], lhsT=ones[:, 0:128], rhs=ones[:], start=True, stop=True)
 
         x_v = x_bytes.rearrange("(p j) k -> p j k", j=NT)
         h_v = h.rearrange("(p j) c -> p j c", j=NT)
@@ -89,13 +97,6 @@ def tile_dienaugrustep_d1p_kernel(tc, x_bytes, x_scale, h, t, wx_words, wx_scale
         uh_v = uh.rearrange("(p s) n -> p s n", s=4)
         wx_v = wx_words[0].rearrange("p n t -> p (n t)")
         un_v = un_words[0].rearrange("p n t -> p (n t)")
-
-        nc.scalar.dma_start(out=xs[:], in_=x_scale.rearrange("(p j) b -> p (j b)", j=NT))
-        for q in range(4):
-            nc.scalar.dma_start(out=wxs[32 * q : 32 * q + 4, :].bitcast(I32), in_=wx_scales[0][4 * q : 4 * q + 4, :].bitcast(I32))
-        nc.scalar.dma_start(out=g_bf[:], in_=g.rearrange("(p s) -> p s", s=4))
-        for q in range(4):
-            nc.scalar.dma_start(out=uns[32 * q : 32 * q + 4, :].bitcast(I32), in_=un_scales[0][4 * q : 4 * q + 4, :].bitcast(I32))
 
         def load_h(q):
             nc.sync.dma_start(out=h_sb[:, 2 * q : 2 * q + 2, :], in_=h_v[:, 2 * q : 2 * q + 2, :])
@@ -117,10 +118,10 @@ def tile_dienaugrustep_d1p_kernel(tc, x_bytes, x_scale, h, t, wx_words, wx_scale
                 load_h(int(name[1]))
             elif name[0] == "t":
                 load_t(0 if name == "t01" else 1)
-            elif name == "uhu":
-                nc.sync.dma_start(out=uhu[:], in_=uh_v[:, :, 0:512])
-            elif name == "uhr":
-                nc.sync.dma_start(out=uhr_raw[:], in_=uh_v[:, :, 512:1024])
+            elif name == "uha":
+                nc.sync.dma_start(out=uh_sb[:, 0:2, :], in_=uh_v[:, 0:2, :])
+            elif name == "uhb":
+                nc.sync.dma_start(out=uh_sb[:, 2:4, :], in_=uh_v[:, 2:4, :])
             elif name == "un":
                 nc.sync.dma_start(out=un[:].bitcast(I32), in_=un_v.bitcast(I32))
             else:
@@ -187,10 +188,12 @@ def tile_dienaugrustep_d1p_kernel(tc, x_bytes, x_scale, h, t, wx_words, wx_scale
             elif op == "QX":
                 nc.vector.quantize_mx(out=xc[:, cols].bitcast(X4), scales=xsc[:, cols], in_=xg[q][:])
             elif op == "PERMa":
-                for s in range(3):
-                    nc.vector.tensor_copy(out=uhr[:, s], in_=uhr_raw[:, s, :].rearrange("p (m c) -> p c m", c=4))
+                for s in range(2):
+                    nc.vector.tensor_copy(out=uhr[:, s], in_=uh_sb[:, s, 512:1024].rearrange("p (m c) -> p c m", c=4))
+            elif op == "PERMc":
+                nc.vector.tensor_copy(out=uhr[:, 2], in_=uh_sb[:, 2, 512:1024].rearrange("p (m c) -> p c m", c=4))
             elif op == "PERMb":
-                nc.scalar.copy(uhr[:, 3], uhr_raw[:, 3, :].rearrange("p (m c) -> p c m", c=4))
+                nc.scalar.copy(uhr[:, 3], uh_sb[:, 3, 512:1024].rearrange("p (m c) -> p c m", c=4))
             elif op == "PERM":
                 nc.vector.tensor_copy(out=g32[:], in_=g_bf[:])
             elif op == "PERMW":
@@ -200,7 +203,7 @@ def tile_dienaugrustep_d1p_kernel(tc, x_bytes, x_scale, h, t, wx_words, wx_scale
                 ps = psum_h.tile([P, D], F32, name="hp", tag="hp")
                 bank["hu", key] = ps
                 for s in range(4):
-                    nc.tensor.matmul(ps[:], lhsT=hT[:, s, 128 * j : 128 * j + 128], rhs=uhu[:, s, :], start=(s == 0), stop=(s == 3))
+                    nc.tensor.matmul(ps[:], lhsT=hT[:, s, 128 * j : 128 * j + 128], rhs=uh_sb[:, s, 0:512], start=(s == 0), stop=(s == 3))
             elif op == "CU":
                 nc.scalar.copy(hu_sb[q][:, i, :], bank["hu", key][:])
             elif op == "HR":

@@ -20,23 +20,23 @@ P = 128
 NT = 8
 NQ = 4
 MANUAL = True
-W_ACT = ["W00","W01","W11","W20","W21","W30","W31"]
+W_ACT = ["W11","W30"]
 IS_ACT = ["IS1","IS2","IS3"]
 D3_GP = []
-LOADS = ["x01","h0","uha","uhb","x23","wx2","h3","h1","wx0","wx1","h2","un","t01","wx3","t23"]
+LOADS = ["h0","x1","x0","x23","uha","uhb","wx0","t0","t1","wx2","t3","h1","un","wx3","wx1","t2","h3","h2"]
 SEQ = (
-    "PERMa PERMc W01 W00 W11 W10 Th0 CH0 PERMb PERM W21 W20 Tx0 CX0 PERMW HU01 "
-    "CU01 HR00 CR00 QX0 HR01 CR01 XR00 AR00 XR01 AR01 XU01 AU01 SR00 S00 SR01 S01 "
-    "Th1 CH1 HU00 CU00 W31 IS0 QS0 XU00 AU00 XA01 AA01 XA00 AA00 W30 Tx1 CX1 "
-    "HR10 CR10 QX1 N00 TN00 DA00 N01 TN01 DA01 SU00 HR11 CR11 XR10 AR10 XR11 AR11 "
-    "SA0 DB00 XU10 SU01 SR10 S10 SR11 S11 HU10 CU10 AU10 Th2 CH2 DB01 XA11 AA11 "
-    "IS1 QS1 XU11 DC00 XA10 AA10 HU11 CU11 AU11 Tx2 CX2 DC01 HR20 CR20 QX2 N10 "
-    "TN10 DA10 N11 TN11 DA11 SU10 HR21 CR21 XR20 AR20 XR21 AR21 SA1 DB10 XU20 SU11 "
-    "SR20 S20 SR21 S21 HU20 CU20 AU20 Th3 CH3 DB11 XA21 AA21 IS2 QS2 XU21 DC10 "
-    "XA20 AA20 HU21 CU21 AU21 Tx3 CX3 DC11 QX3 HR30 CR30 N20 TN20 DA20 N21 TN21 "
-    "DA21 SU20 HR31 CR31 XR30 AR30 XR31 AR31 SA2 DB20 SU21 SR30 S30 SR31 S31 DB21 "
-    "HU30 CU30 XA31 AA31 XU30 AU30 XU31 IS3 QS3 DC20 XA30 AA30 HU31 CU31 AU31 DC21 "
-    "N30 TN30 DA30 N31 TN31 DA31 SU30 SA3 DB30 SU31 DB31 DC30 DC31 "
+    "Th0 W11 W10 W00 CH0 W01 Tx1 W20 W30 Tx0 W21 W31 CX1 PERMa CX0 Tx2 "
+    "QX1 Tx3 QX0 PERMb PERMc HU00 CX2 PERM CX3 XA00 QX2 XA01 CU00 HR00 QX3 AA00 "
+    "PERMW XA31 HR01 CR00 AA01 XR00 AA31 XA10 SA0 CR01 XA11 AR00 XR01 Th1 AA10 SR00 "
+    "XU00 AR01 XU01 CH1 HU01 S00 SR01 AU00 HR10 S01 SU00 AA11 CU01 XR10 IS0 XA20 "
+    "CR10 HR11 AU01 SA1 QS0 XA21 SU01 AR10 N00 CR11 AA20 XR11 SR10 Th2 AA21 TN00 "
+    "XR20 AR11 XR21 CH2 XA30 S10 N01 SR11 DA00 HR20 SA2 S11 TN01 DB00 HR21 IS1 "
+    "AA30 DC00 XU10 CR20 Th3 QS1 CR21 DA01 N10 SA3 AR20 CH3 HU10 AR21 TN10 DB01 "
+    "SR21 HR31 DA10 SR20 DC01 CU10 N11 S20 CR31 HR30 AU10 TN11 S21 SU10 XU20 DA11 "
+    "XR30 CR30 XU30 DB10 XR31 IS2 HU11 AR30 AR31 HU20 SR30 DC10 SR31 QS2 S30 XU11 "
+    "CU11 N20 S31 CU20 HU21 AU11 TN20 AU20 SU11 N21 DA20 SU20 XU21 XU31 DB11 TN21 "
+    "HU30 DB20 CU21 DC11 IS3 HU31 DC20 AU21 CU30 QS3 DA21 SU21 N30 AU30 CU31 N31 "
+    "DB21 TN30 AU31 TN31 DC21 SU31 DA30 SU30 DA31 DB30 DB31 DC30 DC31 "
 )
 
 
@@ -45,8 +45,8 @@ def tile_dienaugrustep_d1p_kernel(tc, x_bytes, x_scale, h, t, wx_words, wx_scale
     with ExitStack() as ctx:
         keep = ctx.enter_context(tc.tile_pool(name="keep", bufs=1))
         work = ctx.enter_context(tc.tile_pool(name="work", bufs=4))
-        psum_t = ctx.enter_context(tc.psum_pool(name="psum_t", bufs=1))
-        psum_h = ctx.enter_context(tc.psum_pool(name="psum_h", bufs=3))
+        psum_t = ctx.enter_context(tc.psum_pool(name="psum_t", bufs=2))
+        psum_h = ctx.enter_context(tc.psum_pool(name="psum_h", bufs=2))
         psum_m = ctx.enter_context(tc.psum_pool(name="psum_m", bufs=4))
         if MANUAL:
             ctx.enter_context(tc.manual_schedule())
@@ -76,8 +76,6 @@ def tile_dienaugrustep_d1p_kernel(tc, x_bytes, x_scale, h, t, wx_words, wx_scale
 
         nc.vector.memset(wxs[:].bitcast(I32), 0)
         nc.scalar.dma_start(out=xs[:], in_=x_scale.rearrange("(p j) b -> p (j b)", j=NT))
-        for q in range(4):
-            nc.scalar.dma_start(out=wxs[32 * q : 32 * q + 4, :].bitcast(I32), in_=wx_scales[0][4 * q : 4 * q + 4, :].bitcast(I32))
         ones = keep.tile([P, 256], BF16, name="ones")
         nc.gpsimd.memset(ones[:], 1.0)
         nc.scalar.activation(warm_out[:], ones[:, 0:1], ACT.Sigmoid)
@@ -113,11 +111,13 @@ def tile_dienaugrustep_d1p_kernel(tc, x_bytes, x_scale, h, t, wx_words, wx_scale
 
         def load(name):
             if name[0] == "x":
-                load_x(0 if name == "x01" else 1)
+                a, b = {"x0": (0, 2), "x1": (2, 4), "x01": (0, 4), "x23": (4, 8)}[name]
+                nc.sync.dma_start(out=x_u8[:, a:b, :], in_=x_v[:, a:b, :])
             elif name[0] == "h":
                 load_h(int(name[1]))
             elif name[0] == "t":
-                load_t(0 if name == "t01" else 1)
+                a, b = {"t0": (0, 2), "t1": (2, 4), "t2": (4, 6), "t3": (6, 8), "t01": (0, 4), "t23": (4, 8)}[name]
+                nc.sync.dma_start(out=t_sb[:, a:b, :], in_=t_v[:, a:b, :])
             elif name == "uha":
                 nc.sync.dma_start(out=uh_sb[:, 0:2, :], in_=uh_v[:, 0:2, :])
             elif name == "uhb":
@@ -129,6 +129,9 @@ def tile_dienaugrustep_d1p_kernel(tc, x_bytes, x_scale, h, t, wx_words, wx_scale
 
         for name in LOADS:
             load(name)
+            if name == "x23":
+                for q in range(4):
+                    nc.sync.dma_start(out=wxs[32 * q : 32 * q + 4, :].bitcast(I32), in_=wx_scales[0][4 * q : 4 * q + 4, :].bitcast(I32))
 
         hu_sb = [keep.tile([P, 2, D], F32, name="hu_sb%d" % q) for q in range(NQ)]
         hr_sb = [keep.tile([P, 2, D], F32, name="hr_sb%d" % q) for q in range(NQ)]

@@ -20,23 +20,23 @@ P = 128
 NT = 8
 NQ = 4
 MANUAL = True
-W_ACT = ["W11","W30"]
-IS_ACT = ["IS1","IS2","IS3"]
-D3_GP = []
-LOADS = ["h0","x1","x0","x23","uha","uhb","wx0","t0","t1","wx2","t3","h1","un","wx3","wx1","t2","h3","h2"]
+W_ACT = ["W10"]
+IS_ACT = ["IS0","IS1","IS2","IS3"]
+LAST = "DC31"
+LOADS = ["h0","x1","x0","x23","uhb","uha","h1","wx2","wx0","t0","wx1","t3","t1","wx3","h2","t2","un","h3"]
 SEQ = (
-    "Th0 W11 W10 W00 CH0 W01 Tx1 W20 W30 Tx0 W21 W31 CX1 PERMa CX0 Tx2 "
-    "QX1 Tx3 QX0 PERMb PERMc HU00 CX2 PERM CX3 XA00 QX2 XA01 CU00 HR00 QX3 AA00 "
-    "PERMW XA31 HR01 CR00 AA01 XR00 AA31 XA10 SA0 CR01 XA11 AR00 XR01 Th1 AA10 SR00 "
-    "XU00 AR01 XU01 CH1 HU01 S00 SR01 AU00 HR10 S01 SU00 AA11 CU01 XR10 IS0 XA20 "
-    "CR10 HR11 AU01 SA1 QS0 XA21 SU01 AR10 N00 CR11 AA20 XR11 SR10 Th2 AA21 TN00 "
-    "XR20 AR11 XR21 CH2 XA30 S10 N01 SR11 DA00 HR20 SA2 S11 TN01 DB00 HR21 IS1 "
-    "AA30 DC00 XU10 CR20 Th3 QS1 CR21 DA01 N10 SA3 AR20 CH3 HU10 AR21 TN10 DB01 "
-    "SR21 HR31 DA10 SR20 DC01 CU10 N11 S20 CR31 HR30 AU10 TN11 S21 SU10 XU20 DA11 "
-    "XR30 CR30 XU30 DB10 XR31 IS2 HU11 AR30 AR31 HU20 SR30 DC10 SR31 QS2 S30 XU11 "
-    "CU11 N20 S31 CU20 HU21 AU11 TN20 AU20 SU11 N21 DA20 SU20 XU21 XU31 DB11 TN21 "
-    "HU30 DB20 CU21 DC11 IS3 HU31 DC20 AU21 CU30 QS3 DA21 SU21 N30 AU30 CU31 N31 "
-    "DB21 TN30 AU31 TN31 DC21 SU31 DA30 SU30 DA31 DB30 DB31 DC30 DC31 "
+    "W10 W11 W00 W01 W30 W21 Th0 CH0 Tx1 CX1 Tx0 CX0 W31 Tx3 W20 Tx2 "
+    "PERMb HU00 PERMc PERMa PERM HR00 QX0 XA01 PERMW XR00 QX1 XA10 CX2 CX3 QX3 XA31 "
+    "QX2 CU00 HR01 AA01 XR01 CR00 AR00 SR00 AA31 CR01 AA10 XA00 AA00 Th1 CH1 AR01 "
+    "SR01 XU00 AU00 SU00 HU01 CU01 S00 S01 IS0 XA11 AA11 SA1 XA20 AA20 XA21 AA21 "
+    "QS0 XR10 HR10 CR10 AR10 HR11 CR11 XU01 AU01 XR11 AR11 SR10 S10 N00 TN00 DA00 "
+    "SR11 S11 Th2 CH2 XA30 AA30 N01 TN01 SA0 DB00 DC00 IS1 QS1 XR20 SA2 XR21 "
+    "DA01 Th3 CH3 HR20 CR20 AR20 SU01 DB01 HR21 CR21 AR21 SR20 S20 N10 TN10 DA10 "
+    "HU10 CU10 SR21 N11 TN11 XU10 AU10 SU10 HR31 CR31 HR30 CR30 DC01 S21 IS2 DA11 "
+    "DB10 XU11 XR31 AR31 SR31 XR30 AR30 SR30 DC10 QS2 S31 HU20 S30 HU11 CU11 AU11 "
+    "CU20 XU20 AU20 N20 TN20 DA20 SU11 DB11 SU20 DB20 DC11 DC20 HU21 CU21 XU31 IS3 "
+    "QS3 N21 TN21 HU31 CU31 XU21 AU21 SU21 DA21 AU31 DB21 HU30 XU30 CU30 AU30 N30 "
+    "TN30 DA30 N31 TN31 DA31 SA3 SU30 DB30 SU31 DB31 DC21 DC30 DC31 "
 )
 
 
@@ -76,14 +76,12 @@ def tile_dienaugrustep_d1p_kernel(tc, x_bytes, x_scale, h, t, wx_words, wx_scale
 
         nc.vector.memset(wxs[:].bitcast(I32), 0)
         nc.scalar.dma_start(out=xs[:], in_=x_scale.rearrange("(p j) b -> p (j b)", j=NT))
+        nc.scalar.dma_start(out=g_bf[:], in_=g.rearrange("(p s) -> p s", s=4))
         ones = keep.tile([P, 256], BF16, name="ones")
         nc.gpsimd.memset(ones[:], 1.0)
         nc.scalar.activation(warm_out[:], ones[:, 0:1], ACT.Sigmoid)
         make_identity(nc, ident[:])
         nc.gpsimd.memset(uns[:].bitcast(I32), 0)
-        nc.gpsimd.dma_start(out=g_bf[:], in_=g.rearrange("(p s) -> p s", s=4))
-        for q in range(4):
-            nc.gpsimd.dma_start(out=uns[32 * q : 32 * q + 4, :].bitcast(I32), in_=un_scales[0][4 * q : 4 * q + 4, :].bitcast(I32))
         wps = psum_t.tile([P, 256], F32, name="tp", tag="tp")
         for k in range(8):
             nc.tensor.matmul(wps[:], lhsT=ones[:, 0:128], rhs=ones[:], start=True, stop=True)
@@ -129,6 +127,9 @@ def tile_dienaugrustep_d1p_kernel(tc, x_bytes, x_scale, h, t, wx_words, wx_scale
 
         for name in LOADS:
             load(name)
+            if name == "un":
+                for q in range(4):
+                    nc.sync.dma_start(out=uns[32 * q : 32 * q + 4, :].bitcast(I32), in_=un_scales[0][4 * q : 4 * q + 4, :].bitcast(I32))
             if name == "x23":
                 for q in range(4):
                     nc.sync.dma_start(out=wxs[32 * q : 32 * q + 4, :].bitcast(I32), in_=wx_scales[0][4 * q : 4 * q + 4, :].bitcast(I32))
@@ -233,7 +234,7 @@ def tile_dienaugrustep_d1p_kernel(tc, x_bytes, x_scale, h, t, wx_words, wx_scale
                     c = 2 * i + w
                     nc.vector.scalar_tensor_tensor(out=su[q][:, c, :], in0=r_sb[q][:, i, 256 * w : 256 * w + 256], scalar=g32[:, c : c + 1], in1=hT[:, c, cols], op0=ALU.mult, op1=ALU.mult)
             elif op == "IS":
-                o, s_ = sg[q][:].rearrange("p (c t) -> p c t", t=4), su[q][:].rearrange("p t c -> p c t")
+                o, s_ = sg[q][:].rearrange("p (c i t) -> p c t i", i=4, t=4), su[q][:].rearrange("p t (c i) -> p c t i", i=4)
                 if name in IS_ACT:
                     nc.scalar.copy(o, s_)
                 else:
@@ -272,11 +273,13 @@ def tile_dienaugrustep_d1p_kernel(tc, x_bytes, x_scale, h, t, wx_words, wx_scale
                 nc.vector.scalar_tensor_tensor(out=part["e", key][:], in0=part["d", key][:], scalar=att[:, j : j + 1], in1=u_sb[q][:, i, :], op0=ALU.mult, op1=ALU.mult)
             elif op == "DC":
                 o = work.tile([P, D], F32, name="o")
-                if name in D3_GP:
-                    nc.gpsimd.tensor_tensor(out=o[:], in0=part["e", key][:], in1=h_sb[:, j, :], op=ALU.add)
-                else:
-                    nc.vector.tensor_tensor(out=o[:], in0=part["e", key][:], in1=h_sb[:, j, :], op=ALU.add)
-                nc.sync.dma_start(out=o_v[:, j, :], in_=o[:])
+                if True:
+                    n_piece = 2 if name == LAST else 1
+                    w_piece = D // n_piece
+                    for c in range(n_piece):
+                        part_cols = slice(w_piece * c, w_piece * c + w_piece)
+                        nc.vector.tensor_tensor(out=o[:, part_cols], in0=part["e", key][:, part_cols], in1=h_sb[:, j, part_cols], op=ALU.add)
+                        nc.sync.dma_start(out=o_v[:, j, part_cols], in_=o[:, part_cols])
 
         for name in SEQ.split():
             emit(name)

from contextlib import ExitStack

import concourse.mybir as mybir
from concourse.masks import make_identity

B, DI, D = 1024, 512, 512
FLOPS = 2 * B * DI * 4 * D + 2 * B * D * 2 * D + 2 * B * D * D

F32 = mybir.dt.float32
BF16 = mybir.dt.bfloat16
I32 = mybir.dt.int32
U32 = mybir.dt.uint32
U8 = mybir.dt.uint8
FP8 = mybir.dt.float8_e4m3fn
X4 = mybir.dt.float8_e4m3fn_x4
ALU = mybir.AluOpType
ACT = mybir.ActivationFunctionType

P = 128
NT = 8
NQ = 4
MANUAL = True
W_ACT = ["W10"]
IS_ACT = ["IS0","IS1","IS2","IS3"]
LAST = "DC31"
LOADS = ["h0","x1","x0","x23","uhb","uha","h1","wx2","wx0","t0","wx1","t3","t1","wx3","h2","t2","un","h3"]
SEQ = (
    "W10 W11 W00 W01 W30 W21 Th0 CH0 Tx1 CX1 Tx0 CX0 W31 Tx3 W20 Tx2 "
    "PERMb HU00 PERMc PERMa PERM HR00 QX0 XA01 PERMW XR00 QX1 XA10 CX2 CX3 QX3 XA31 "
    "QX2 CU00 HR01 AA01 XR01 CR00 AR00 SR00 AA31 CR01 AA10 XA00 AA00 Th1 CH1 AR01 "
    "SR01 XU00 AU00 SU00 HU01 CU01 S00 S01 IS0 XA11 AA11 SA1 XA20 AA20 XA21 AA21 "
    "QS0 XR10 HR10 CR10 AR10 HR11 CR11 XU01 AU01 XR11 AR11 SR10 S10 N00 TN00 DA00 "
    "SR11 S11 Th2 CH2 XA30 AA30 N01 TN01 SA0 DB00 DC00 IS1 QS1 XR20 SA2 XR21 "
    "DA01 Th3 CH3 HR20 CR20 AR20 SU01 DB01 HR21 CR21 AR21 SR20 S20 N10 TN10 DA10 "
    "HU10 CU10 SR21 N11 TN11 XU10 AU10 SU10 HR31 CR31 HR30 CR30 DC01 S21 IS2 DA11 "
    "DB10 XU11 XR31 AR31 SR31 XR30 AR30 SR30 DC10 QS2 S31 HU20 S30 HU11 CU11 AU11 "
    "CU20 XU20 AU20 N20 TN20 DA20 SU11 DB11 SU20 DB20 DC11 DC20 HU21 CU21 XU31 IS3 "
    "QS3 N21 TN21 HU31 CU31 XU21 AU21 SU21 DA21 AU31 DB21 HU30 XU30 CU30 AU30 N30 "
    "TN30 DA30 N31 TN31 DA31 SA3 SU30 DB30 SU31 DB31 DC21 DC30 DC31 "
)


def tile_dienaugrustep_d1p_kernel(tc, x_bytes, x_scale, h, t, wx_words, wx_scales, uh, g, un_words, un_scales, out):
    nc = tc.nc
    with ExitStack() as ctx:
        keep = ctx.enter_context(tc.tile_pool(name="keep", bufs=1))
        work = ctx.enter_context(tc.tile_pool(name="work", bufs=4))
        psum_t = ctx.enter_context(tc.psum_pool(name="psum_t", bufs=2))
        psum_h = ctx.enter_context(tc.psum_pool(name="psum_h", bufs=2))
        psum_m = ctx.enter_context(tc.psum_pool(name="psum_m", bufs=4))
        if MANUAL:
            ctx.enter_context(tc.manual_schedule())

        ident = keep.tile([P, P], F32, name="ident")
        warm_out = keep.tile([P, 1], F32, name="warm_out")
        xs = keep.tile([P, NT * 4], F32, name="xs")
        x_u8 = keep.tile([P, NT, DI], U8, name="x_u8")
        xb = keep.tile([P, NT, DI], BF16, name="xb", align_bytes=64)
        xc = keep.tile([P, B], U32, name="xc", align_bytes=64)
        xsc = keep.tile([P, B], U8, name="xsc", align_bytes=64)
        h_sb = keep.tile([P, NT, D], BF16, name="h_sb")
        t_sb = keep.tile([P, NT, D], BF16, name="t_sb")
        hT = keep.tile([P, 4, B], BF16, name="hT")
        uh_sb = keep.tile([P, 4, 2 * D], BF16, name="uh_sb")
        uhr = keep.tile([P, 4, 4, P], BF16, name="uhr")
        wx = [keep.tile([P, 512], U32, name="wx%d" % b, align_bytes=64) for b in range(4)]
        wxs = keep.tile([P, 2048], U8, name="wxs", align_bytes=64)
        wr = keep.tile([P, 512], U32, name="wr", align_bytes=64)
        wrs = keep.tile([P, 512], U8, name="wrs", align_bytes=64)
        un = keep.tile([P, 512], U32, name="un", align_bytes=64)
        uns = keep.tile([P, 512], U8, name="uns", align_bytes=64)
        g_bf = keep.tile([P, 4], BF16, name="g_bf")
        g32 = keep.tile([P, 4], F32, name="g32")
        dot = keep.tile([P, NT], F32, name="dot")
        att = keep.tile([P, NT], F32, name="att")

        nc.vector.memset(wxs[:].bitcast(I32), 0)
        nc.scalar.dma_start(out=xs[:], in_=x_scale.rearrange("(p j) b -> p (j b)", j=NT))
        nc.scalar.dma_start(out=g_bf[:], in_=g.rearrange("(p s) -> p s", s=4))
        ones = keep.tile([P, 256], BF16, name="ones")
        nc.gpsimd.memset(ones[:], 1.0)
        nc.scalar.activation(warm_out[:], ones[:, 0:1], ACT.Sigmoid)
        make_identity(nc, ident[:])
        nc.gpsimd.memset(uns[:].bitcast(I32), 0)
        wps = psum_t.tile([P, 256], F32, name="tp", tag="tp")
        for k in range(8):
            nc.tensor.matmul(wps[:], lhsT=ones[:, 0:128], rhs=ones[:], start=True, stop=True)

        x_v = x_bytes.rearrange("(p j) k -> p j k", j=NT)
        h_v = h.rearrange("(p j) c -> p j c", j=NT)
        t_v = t.rearrange("(p j) c -> p j c", j=NT)
        o_v = out.rearrange("(p j) c -> p j c", j=NT)
        uh_v = uh.rearrange("(p s) n -> p s n", s=4)
        wx_v = wx_words[0].rearrange("p n t -> p (n t)")
        un_v = un_words[0].rearrange("p n t -> p (n t)")

        def load_h(q):
            nc.sync.dma_start(out=h_sb[:, 2 * q : 2 * q + 2, :], in_=h_v[:, 2 * q : 2 * q + 2, :])

        def load_t(k):
            nc.sync.dma_start(out=t_sb[:, 4 * k : 4 * k + 4, :], in_=t_v[:, 4 * k : 4 * k + 4, :])

        def load_x(k):
            nc.sync.dma_start(out=x_u8[:, 4 * k : 4 * k + 4, :], in_=x_v[:, 4 * k : 4 * k + 4, :])

        def load_w(b):
            nc.sync.dma_start(out=wx[b][:].bitcast(I32), in_=wx_v[:, 2048 * b : 2048 * b + 2048].bitcast(I32))


        def load(name):
            if name[0] == "x":
                a, b = {"x0": (0, 2), "x1": (2, 4), "x01": (0, 4), "x23": (4, 8)}[name]
                nc.sync.dma_start(out=x_u8[:, a:b, :], in_=x_v[:, a:b, :])
            elif name[0] == "h":
                load_h(int(name[1]))
            elif name[0] == "t":
                a, b = {"t0": (0, 2), "t1": (2, 4), "t2": (4, 6), "t3": (6, 8), "t01": (0, 4), "t23": (4, 8)}[name]
                nc.sync.dma_start(out=t_sb[:, a:b, :], in_=t_v[:, a:b, :])
            elif name == "uha":
                nc.sync.dma_start(out=uh_sb[:, 0:2, :], in_=uh_v[:, 0:2, :])
            elif name == "uhb":
                nc.sync.dma_start(out=uh_sb[:, 2:4, :], in_=uh_v[:, 2:4, :])
            elif name == "un":
                nc.sync.dma_start(out=un[:].bitcast(I32), in_=un_v.bitcast(I32))
            else:
                load_w(int(name[2]))

        for name in LOADS:
            load(name)
            if name == "un":
                for q in range(4):
                    nc.sync.dma_start(out=uns[32 * q : 32 * q + 4, :].bitcast(I32), in_=un_scales[0][4 * q : 4 * q + 4, :].bitcast(I32))
            if name == "x23":
                for q in range(4):
                    nc.sync.dma_start(out=wxs[32 * q : 32 * q + 4, :].bitcast(I32), in_=wx_scales[0][4 * q : 4 * q + 4, :].bitcast(I32))

        hu_sb = [keep.tile([P, 2, D], F32, name="hu_sb%d" % q) for q in range(NQ)]
        hr_sb = [keep.tile([P, 2, D], F32, name="hr_sb%d" % q) for q in range(NQ)]
        u_sb = [keep.tile([P, 2, D], F32, name="u_sb%d" % q) for q in range(NQ)]
        r_sb = [keep.tile([P, 2, D], F32, name="r_sb%d" % q) for q in range(NQ)]
        su = [keep.tile([P, 4, 256], BF16, name="su%d" % q) for q in range(NQ)]
        sg = [keep.tile([P, 1024], BF16, name="sg%d" % q, align_bytes=64) for q in range(NQ)]
        xg = [keep.tile([P, 1024], BF16, name="xg%d" % q, align_bytes=64) for q in range(NQ)]
        sc = [keep.tile([P, 256], U32, name="sc%d" % q, align_bytes=64) for q in range(NQ)]
        ss = [keep.tile([P, 256], U8, name="ss%d" % q, align_bytes=64) for q in range(NQ)]
        bank, part = {}, {}

        def transposes(src, q):
            pt = psum_t.tile([P, 2, 2, P], F32, name="tp", tag="tp")
            for i in range(2):
                words = src[:, 2 * q + i, :].bitcast(F32)
                for u in range(2):
                    nc.tensor.transpose(pt[:, i, u, :], words[:, u:256:2], ident[:])
            return pt

        def x_block(ps, j, b, start, stop):
            tok = slice(128 * j, 128 * j + 128)
            nc.tensor.matmul_mx(ps[:], lhsT=xc[:, tok].bitcast(X4), lhsT_scale=xsc[:, tok], rhs=wx[b][:].bitcast(X4), rhs_scale=wxs[:, 512 * b : 512 * b + 512], start=start, stop=stop)

        def mxbank():
            return psum_m.tile([P, D], F32, name="mx", tag="mx")

        def emit(name):
            op = "".join([c for c in name if c not in "0123456789"])
            dig = name[len(op):]
            q = int(dig[0]) if dig else 0
            i = int(dig[1]) if len(dig) > 1 else 0
            j = 2 * q + i
            cols = slice(256 * q, 256 * q + 256)
            key = (q, i)
            if op == "Th":
                bank["h", q] = transposes(h_sb, q)
            elif op == "CH":
                pt = bank["h", q]
                pv = pt[:].rearrange("p i u r -> p (i u r)").bitcast(BF16).rearrange("p (i u r e) -> p u e i r", i=2, u=2, e=2)
                for u in range(2):
                    o = hT[:, 2 * u : 2 * u + 2, cols].rearrange("p e (i r) -> p e i r", i=2)
                    nc.scalar.copy(o, pv[:, u])
            elif op == "W":
                for b in range(4):
                    src = x_u8[:, j, 128 * b : 128 * b + 128].bitcast(FP8)
                    dst = xb[:, j, 128 * b : 128 * b + 128]
                    sca = xs[:, 4 * j + b : 4 * j + b + 1]
                    if name in W_ACT:
                        nc.scalar.activation(dst, src, ACT.Copy, scale=sca)
                    else:
                        nc.vector.tensor_scalar(out=dst, in0=src, scalar1=sca, scalar2=None, op0=ALU.mult)
            elif op == "Tx":
                bank["x", q] = transposes(xb, q)
            elif op == "CX":
                nc.scalar.copy(xg[q][:].bitcast(F32).rearrange("p (i r u) -> p i r u", i=2, u=2), bank["x", q][:].rearrange("p i u r -> p i r u"))
            elif op == "QX":
                nc.vector.quantize_mx(out=xc[:, cols].bitcast(X4), scales=xsc[:, cols], in_=xg[q][:])
            elif op == "PERMa":
                for s in range(2):
                    nc.vector.tensor_copy(out=uhr[:, s], in_=uh_sb[:, s, 512:1024].rearrange("p (m c) -> p c m", c=4))
            elif op == "PERMc":
                nc.vector.tensor_copy(out=uhr[:, 2], in_=uh_sb[:, 2, 512:1024].rearrange("p (m c) -> p c m", c=4))
            elif op == "PERMb":
                nc.scalar.copy(uhr[:, 3], uh_sb[:, 3, 512:1024].rearrange("p (m c) -> p c m", c=4))
            elif op == "PERM":
                nc.vector.tensor_copy(out=g32[:], in_=g_bf[:])
            elif op == "PERMW":
                nc.vector.tensor_copy(out=wr[:].bitcast(I32).rearrange("p (c m) -> p c m", c=4), in_=wx[2][:].bitcast(I32).rearrange("p (m c) -> p c m", c=4))
                nc.vector.tensor_copy(out=wrs[:].rearrange("p (c m) -> p m c", c=4), in_=wxs[:, 1024:1536].rearrange("p (m c) -> p m c", c=4))
            elif op == "HU":
                ps = psum_h.tile([P, D], F32, name="hp", tag="hp")
                bank["hu", key] = ps
                for s in range(4):
                    nc.tensor.matmul(ps[:], lhsT=hT[:, s, 128 * j : 128 * j + 128], rhs=uh_sb[:, s, 0:512], start=(s == 0), stop=(s == 3))
            elif op == "CU":
                nc.scalar.copy(hu_sb[q][:, i, :], bank["hu", key][:])
            elif op == "HR":
                ps = psum_h.tile([P, D], F32, name="hp", tag="hp")
                bank["hr", key] = ps
                for w in range(2):
                    for s in range(4):
                        nc.tensor.matmul(ps[:, 256 * w : 256 * w + 256], lhsT=uhr[:, s, 2 * i + w, :], rhs=hT[:, s, cols], start=(s == 0), stop=(s == 3))
            elif op == "CR":
                nc.scalar.copy(hr_sb[q][:, i, :], bank["hr", key][:])
            elif op == "XR":
                ps = mxbank()
                bank["xr", key] = ps
                for w in range(2):
                    ch = slice(128 * (2 * i + w), 128 * (2 * i + w) + 128)
                    nc.tensor.matmul_mx(ps[:, 256 * w : 256 * w + 256], lhsT=wr[:, ch].bitcast(X4), lhsT_scale=wrs[:, ch], rhs=xc[:, cols].bitcast(X4), rhs_scale=xsc[:, cols], start=True, stop=True)
            elif op == "AR":
                part["rp", key] = work.tile([P, D], F32, name="rp")
                nc.vector.tensor_tensor(out=part["rp", key][:], in0=bank["xr", key][:], in1=hr_sb[q][:, i, :], op=ALU.add)
            elif op == "SR":
                nc.scalar.activation(r_sb[q][:, i, :], part["rp", key][:], ACT.Sigmoid)
            elif op == "S":
                for w in range(2):
                    c = 2 * i + w
                    nc.vector.scalar_tensor_tensor(out=su[q][:, c, :], in0=r_sb[q][:, i, 256 * w : 256 * w + 256], scalar=g32[:, c : c + 1], in1=hT[:, c, cols], op0=ALU.mult, op1=ALU.mult)
            elif op == "IS":
                o, s_ = sg[q][:].rearrange("p (c i t) -> p c t i", i=4, t=4), su[q][:].rearrange("p t (c i) -> p c t i", i=4)
                if name in IS_ACT:
                    nc.scalar.copy(o, s_)
                else:
                    nc.vector.tensor_copy(out=o, in_=s_)
            elif op == "QS":
                nc.vector.quantize_mx(out=sc[q][:].bitcast(X4), scales=ss[q][:], in_=sg[q][:])
            elif op == "XU":
                bank["xu", key] = mxbank()
                x_block(bank["xu", key], j, 1, True, True)
            elif op == "AU":
                part["up", key] = work.tile([P, D], F32, name="up")
                nc.vector.tensor_tensor(out=part["up", key][:], in0=bank["xu", key][:], in1=hu_sb[q][:, i, :], op=ALU.add)
            elif op == "SU":
                nc.scalar.activation(u_sb[q][:, i, :], part["up", key][:], ACT.Sigmoid)
            elif op == "XA":
                bank["xa", key] = mxbank()
                x_block(bank["xa", key], j, 0, True, True)
            elif op == "AA":
                prod = work.tile([P, D], F32, name="prod")
                nc.vector.scalar_tensor_tensor(out=prod[:], in0=bank["xa", key][:], scalar=1.0, in1=t_sb[:, j, :], op0=ALU.mult, op1=ALU.mult, accum_out=dot[:, j : j + 1])
            elif op == "SA":
                nc.scalar.activation(att[:, 2 * q : 2 * q + 2], dot[:, 2 * q : 2 * q + 2], ACT.Sigmoid, scale=1.0 / (512.0**0.5))
            elif op == "N":
                bank["n", key] = mxbank()
                x_block(bank["n", key], j, 3, True, False)
                tok = slice(128 * i, 128 * i + 128)
                nc.tensor.matmul_mx(bank["n", key][:], lhsT=sc[q][:, tok].bitcast(X4), lhsT_scale=ss[q][:, tok], rhs=un[:].bitcast(X4), rhs_scale=uns[:], start=False, stop=True)
            elif op == "TN":
                part["n", key] = work.tile([P, D], F32, name="n")
                nc.scalar.activation(part["n", key][:], bank["n", key][:], ACT.Tanh)
            elif op == "DA":
                part["d", key] = work.tile([P, D], F32, name="d")
                nc.vector.tensor_tensor(out=part["d", key][:], in0=part["n", key][:], in1=h_sb[:, j, :], op=ALU.subtract)
            elif op == "DB":
                part["e", key] = work.tile([P, D], F32, name="e")
                nc.vector.scalar_tensor_tensor(out=part["e", key][:], in0=part["d", key][:], scalar=att[:, j : j + 1], in1=u_sb[q][:, i, :], op0=ALU.mult, op1=ALU.mult)
            elif op == "DC":
                o = work.tile([P, D], F32, name="o")
                if True:
                    n_piece = 2 if name == LAST else 1
                    w_piece = D // n_piece
                    for c in range(n_piece):
                        part_cols = slice(w_piece * c, w_piece * c + w_piece)
                        nc.vector.tensor_tensor(out=o[:, part_cols], in0=part["e", key][:, part_cols], in1=h_sb[:, j, part_cols], op=ALU.add)
                        nc.sync.dma_start(out=o_v[:, j, part_cols], in_=o[:, part_cols])

        for name in SEQ.split():
            emit(name)
